import numpy as np
import ml_dtypes


def mxq(x, axis, fmt="e4m3"):
    dtype, down = {"e4m3": (ml_dtypes.float8_e4m3fn, 7), "e5m2": (ml_dtypes.float8_e5m2, 14)}[fmt]
    v = np.moveaxis(np.asarray(x, np.float32).astype(ml_dtypes.bfloat16).astype(np.float64), axis, -1)
    blocks = v.reshape(v.shape[:-1] + (-1, 32))
    amax = np.abs(blocks).max(-1, keepdims=True)
    byte = np.maximum(np.where(amax > 0, np.frexp(amax)[1] - 1 + 127, 0) - down, 1)
    scale = np.exp2(byte - 127.0)
    codes = (blocks / scale).astype(np.float32).astype(dtype).astype(np.float64)
    return np.moveaxis((codes * scale).reshape(v.shape), -1, axis)


WIDE = False


def mx_kscale(k):
    if not WIDE:
        return np.ones(k)
    levels = np.array([10, -10, 5, -5, 0])
    if k % 512:
        return np.exp2(np.random.permutation(np.resize(levels, k // 32))).repeat(32)
    a = np.empty((k // 512, 16))
    for p in range(k // 512):
        a[p, :8] = np.random.permutation(np.resize(levels, 8))
        for g in range(8):
            far = levels[np.abs(levels - a[p, g]) >= 10]
            a[p, g + 8] = far[np.random.randint(len(far))]
    return np.exp2(a.ravel()).repeat(32)


def f64(x):
    return np.asarray(x).astype(np.float64)


def striped(idx):
    return np.tile(idx.reshape(-1, 16).T, (8, 1)).astype(np.uint16)


def unstriped(offs):
    return offs[:16].T.reshape(-1).astype(np.int64)


E2M1 = np.array([0.0, 0.5, 1.0, 1.5, 2.0, 3.0, 4.0, 6.0, -0.0, -0.5, -1.0, -1.5, -2.0, -3.0, -4.0, -6.0])


def pack_weight(w, fmt):
    k, n = w.shape
    w = f64(np.asarray(w, np.float32).astype(ml_dtypes.bfloat16)).reshape(k // 32, 32, n)
    amax = np.abs(w).max(1)
    if fmt == "e4m3":
        byte = np.frexp(amax)[1] - 1 + 127 - 7
    else:
        mant, ex = np.frexp(amax / 6.0)
        byte = np.where(mant > 0.5, ex, ex - 1) + 127
    byte = np.clip(np.where(amax > 0, byte, 1), 1, 254)
    scaled = (w * np.exp2(127.0 - byte)[:, None, :]).reshape(k, n).astype(np.float32)
    by_word = np.ascontiguousarray(scaled.reshape(k // 512, 128, 4, n).transpose(0, 1, 3, 2))
    if fmt == "e4m3":
        words = by_word.astype(ml_dtypes.float8_e4m3fn).view(np.uint8)
    else:
        c = by_word.astype(ml_dtypes.float4_e2m1fn).view(np.uint8) & 0xF
        words = (c[..., 0::2] | (c[..., 1::2] << 4)).reshape(k // 512, 128, 2 * n)
    return np.ascontiguousarray(words), np.ascontiguousarray(byte.astype(np.uint8).reshape(k // 512, 16, n))


def unpack_weight(words, scales, fmt):
    g, _, n = scales.shape
    words = np.ascontiguousarray(words).reshape(g, 128, n, -1)
    if fmt == "e4m3":
        vals = words.view(ml_dtypes.float8_e4m3fn).astype(np.float64)
    else:
        nib = np.empty((g, 128, n, 4), np.uint8)
        nib[..., 0::2] = words & 0xF
        nib[..., 1::2] = words >> 4
        vals = E2M1[nib]
    vals = vals * np.repeat(np.exp2(scales.astype(np.float64) - 127.0), 8, axis=1)[..., None]
    return vals.transpose(0, 1, 3, 2).reshape(g * 512, n)


def gelu(v):
    return 0.5 * v * (1.0 + np.tanh(np.sqrt(2.0 / np.pi) * (v + 0.044715 * v**3)))


def bf(x):
    return np.asarray(x, np.float32).astype(ml_dtypes.bfloat16)


def planes(Y):
    n, m = Y.shape
    b = f64(bf(Y)).reshape(n // 32, 32, m)
    amax = np.abs(b).max(1)
    byte = np.clip(np.where(amax > 0, np.frexp(amax)[1] - 1 + 127 - 7, 1), 1, 254)
    codes = (b * np.exp2(127.0 - byte)[:, None, :]).reshape(n, m).astype(np.float32).astype(ml_dtypes.float8_e4m3fn).view(np.uint8)
    words = codes.reshape(n // 512, 128, 4, m).transpose(0, 1, 3, 2)
    return np.ascontiguousarray(words), np.ascontiguousarray(byte.astype(np.uint8).reshape(n // 512, 16, m))


K, T, S, H, N, P = 1024, 4096, 1024, 512, 1024, 512


def setup_inputs():
    n = np.random.standard_normal
    s = mx_kscale(K)[:, None]
    u = mx_kscale(H)[:, None]
    tab_words, tab_scales = pack_weight(n((K, T)) * s, "e4m3")
    w1 = n((K, H)) / np.sqrt(K) / s * u.T
    b1 = 0.5 * n(H) * u[:, 0]
    wa_words, wa_scales = pack_weight(0.75 * n((H, N)) / np.sqrt(H) / u, "e2m1")
    wb_words, wb_scales = pack_weight(0.55 * n((K, N)) / np.sqrt(K) / s, "e4m3")
    level = np.exp(0.8 * n(N))
    return {
        "tab_words": tab_words, "tab_scales": tab_scales,
        "offs": striped(np.random.permutation(T)[:S]),
        "pos1": striped(np.random.permutation(S)[:P]),
        "pos2": striped(np.random.permutation(S)[:P]),
        "w1": w1.astype(np.float32), "b1": b1.astype(np.float32),
        "wa_words": wa_words, "wa_scales": wa_scales,
        "wb_words": wb_words, "wb_scales": wb_scales,
        "temp": np.random.uniform(0.4, 1.6, N).astype(np.float32),
        "ga": (level * np.random.uniform(3.0, 6.0, N)).astype(np.float32),
        "gc": (level * np.random.uniform(0.3, 0.9, N)).astype(np.float32),
    }


def reference(tab_words, tab_scales, offs, pos1, pos2, w1, b1, wa_words, wa_scales,
              wb_words, wb_scales, temp, ga, gc):
    v = unpack_weight(tab_words, tab_scales, "e4m3")[:, unstriped(offs)]
    wa = unpack_weight(wa_words, wa_scales, "e2m1")
    wb = unpack_weight(wb_words, wb_scales, "e4m3")
    h = np.maximum((mxq(f64(w1), 0, "e4m3").T @ v) + f64(b1)[:, None], 0.0)
    hq = mxq(h, 0, "e4m3")
    e = wa.T @ hq + wb.T @ v
    top = e.max(axis=1)
    a = np.exp(f64(temp)[:, None] * (e[:, unstriped(pos1)] - top[:, None]))
    c = e[:, unstriped(pos2)]
    y = f64(ga)[:, None] * a * c + f64(gc)[:, None] * c
    words, scales = planes(y)
    return y, words, scales

@@ -1,0 +1,294 @@
+from contextlib import ExitStack
+
+import concourse.mybir as mybir
+
+K, T, S, H, N, M = 1024, 4096, 1024, 512, 1024, 512
+FLOPS = 2 * (K * H * S + H * N * S + K * N * S)
+
+F32 = mybir.dt.float32
+BF16 = mybir.dt.bfloat16
+I32 = mybir.dt.int32
+U32 = mybir.dt.uint32
+U16 = mybir.dt.uint16
+U8 = mybir.dt.uint8
+FP8X4 = mybir.dt.float8_e4m3fn_x4
+FP4X4 = mybir.dt.float4_e2m1fn_x4
+ALU = mybir.AluOpType
+ACT = mybir.ActivationFunctionType
+
+P = 128
+BANK = 512
+TILES = N // P
+LAG = 2
+
+
+def tile_list_page_flush_adviser_kernel(
+    tc, tab_words, tab_scales, offs, pos1, pos2, w1, b1, wa_words, wa_scales,
+    wb_words, wb_scales, temp, ga, gc, out_0, out_1, out_2,
+):
+    nc = tc.nc
+    with ExitStack() as ctx:
+        keep = ctx.enter_context(tc.tile_pool(name="keep", bufs=1))
+        ring = ctx.enter_context(tc.tile_pool(name="ring", bufs=3))
+        psum = ctx.enter_context(tc.psum_pool(name="psum", bufs=8))
+
+        def held(shape, dtype, name, after=None):
+            return keep.tile(shape, dtype, name=name, tag=after or name, align_bytes=64)
+
+        idx = held([P, S // 16], U16, "idx")
+        p1 = held([P, M // 16], U16, "p1")
+        p2 = held([P, M // 16], U16, "p2")
+        b1_sb = held([P, 4], F32, "b1_sb")
+        temp_sb = held([P, TILES], F32, "temp_sb")
+        ga_sb = held([P, TILES], F32, "ga_sb")
+        gc_sb = held([P, TILES], F32, "gc_sb")
+        tab_w = [held([P, T], U32, f"tab_w{a}") for a in range(2)]
+        tab_s = held([P, T], U8, "tab_s")
+        w_s_raw = held([P, N], U8, "w_s_raw")
+        w1_raw0 = held([P, 4, H], F32, "w1_raw0")
+        wb_raw = [held([P, N], U32, f"wb_raw{a}") for a in range(2)]
+        wa_raw = held([P, N], U16, "wa_raw")
+
+        nc.vector.memset(tab_s[:].bitcast(I32), 0)
+        nc.gpsimd.memset(w_s_raw[:].bitcast(I32), 0)
+
+        nc.sync.dma_start(idx[:], offs)
+
+        def load_rows(dst, src):
+            nc.sync.dma_start(
+                dst[:].rearrange("p (g t) -> p g t", t=4),
+                src.rearrange("(g p t) -> p g t", p=P, t=4),
+            )
+
+        load_rows(temp_sb, temp)
+        load_rows(b1_sb, b1)
+        nc.sync.dma_start(p1[:], pos1)
+
+        def load_words(dst, src):
+            nc.sync.dma_start(dst[:].bitcast(I32), src.rearrange("p c i -> p (c i)").bitcast(I32))
+
+        load_words(tab_w[0], tab_words[0])
+        for q in range(4):
+            nc.sync.dma_start(
+                tab_s[32 * q : 32 * q + 8, :].bitcast(I32),
+                tab_scales[:, 4 * q : 4 * q + 4, :].bitcast(I32),
+            )
+        nc.sync.dma_start(w1_raw0[:], w1[0:512, :].rearrange("(p j) c -> p j c", j=4))
+        load_words(tab_w[1], tab_words[1])
+
+        def load_w1_half(c):
+            raw = held([P, 4, H // 2], F32, f"w1_raw1{c}")
+            nc.sync.dma_start(
+                raw[:], w1[512:1024, 256 * c : 256 * (c + 1)].rearrange("(p j) c -> p j c", j=4)
+            )
+            return raw
+
+        w1_raw1 = [load_w1_half(0), load_w1_half(1)]
+        for a in range(2):
+            load_words(wb_raw[a], wb_words[a])
+        nc.sync.dma_start(wa_raw[:].bitcast(I32), wa_words[0].bitcast(I32))
+        nc.sync.dma_start(p2[:], pos2)
+        load_rows(ga_sb, ga)
+        load_rows(gc_sb, gc)
+        for q in range(4):
+            nc.gpsimd.dma_start(
+                w_s_raw[32 * q : 32 * q + 4, :].bitcast(I32),
+                wa_scales[0, 4 * q : 4 * q + 4, :].bitcast(I32),
+            )
+            nc.gpsimd.dma_start(
+                w_s_raw[32 * q + 4 : 32 * q + 12, :].bitcast(I32),
+                wb_scales[:, 4 * q : 4 * q + 4, :].bitcast(I32),
+            )
+
+        neg_temp = held([P, TILES], F32, "neg_temp")
+        nc.vector.tensor_scalar(neg_temp[:], temp_sb[:], -1.0, None, ALU.mult)
+
+        v_w = [held([P, S], U32, "v_w0")]
+        v_s = held([P, S], U8, "v_s")
+        nc.vector.tensor_copy(v_w[0][:], tab_w[0][:].indirect(idx[:]))
+        nc.vector.tensor_copy(v_s[:], tab_s[:].indirect(idx[:]))
+
+        w1_w = [held([P, H], U32, f"w1_w{a}") for a in range(2)]
+        w1_s = [held([P, H], U8, f"w1_s{a}") for a in range(2)]
+
+        def w1_views(bf, raw):
+            return (
+                bf[:].rearrange("p (t m j) -> p m t j", t=4, j=4),
+                raw[:].rearrange("p j (m t) -> p m t j", t=4),
+            )
+
+        w1_bf0 = held([P, 4 * H], BF16, "w1_bf0")
+        nc.scalar.copy(*w1_views(w1_bf0, w1_raw0))
+        nc.vector.quantize_mx(w1_w[0][:].bitcast(FP8X4), w1_s[0][:], w1_bf0[:])
+
+        v_w.append(held([P, S], U32, "v_w1", "w1_bf0"))
+        nc.vector.tensor_copy(v_w[1][:], tab_w[1][:].indirect(idx[:]))
+        w1_bf1 = [held([P, 2 * H], BF16, "w1_bf10"), held([P, 2 * H], BF16, "w1_bf11", "tab_w1")]
+        nc.scalar.copy(*w1_views(w1_bf1[0], w1_raw1[0]))
+        nc.vector.tensor_copy(*w1_views(w1_bf1[1], w1_raw1[1]))
+        for c in range(2):
+            for t in range(4):
+                cols = slice(P * t + 64 * c, P * t + 64 * (c + 1))
+                nc.vector.quantize_mx(
+                    w1_w[1][:, cols].bitcast(FP8X4), w1_s[1][:, cols], w1_bf1[c][:, 256 * t : 256 * (t + 1)]
+                )
+
+        w_s = held([P, N], U8, "w_s", "tab_w1")
+        nc.vector.tensor_copy(
+            w_s[:].rearrange("p (g t c i) -> p g c t i", g=2, t=4, i=16),
+            w_s_raw[:].rearrange("p (g c i t) -> p g c t i", g=2, t=4, i=16),
+        )
+
+        def v_operand(a, half):
+            cols = slice(BANK * half, BANK * (half + 1))
+            return dict(rhs=v_w[a][:, cols].bitcast(FP8X4), rhs_scale=v_s[4 * a : P, cols])
+
+        h_acc = [[psum.tile([P, BANK], F32, name="acc") for t in range(4)] for half in range(2)]
+        for a in range(2):
+            for half in range(2):
+                for t in range(4):
+                    cols = slice(P * t, P * (t + 1))
+                    nc.tensor.matmul_mx(
+                        out=h_acc[half][t][:],
+                        lhsT=w1_w[a][:, cols].bitcast(FP8X4),
+                        lhsT_scale=w1_s[a][:, cols],
+                        start=(a == 0),
+                        stop=(a == 1),
+                        **v_operand(a, half),
+                    )
+        h_w = [held([P, BANK], U32, f"h_w{half}") for half in range(2)]
+        h_s = [held([P, BANK], U8, f"h_s{half}") for half in range(2)]
+        h_rows = [held([P, 4, BANK], BF16, f"h_rows{half}") for half in range(2)]
+        h_bf = [held([P, 4 * BANK], BF16, f"h_bf{half}") for half in range(2)]
+        for half in range(2):
+            for t in range(4):
+                if half == 0 and t % 2 == 1:
+                    nc.vector.tensor_scalar(
+                        h_rows[half][:, t, :], h_acc[half][t][:], b1_sb[:, t : t + 1], 0.0, ALU.add, ALU.max
+                    )
+                else:
+                    nc.scalar.activation(
+                        h_rows[half][:, t, :], h_acc[half][t][:], ACT.Relu, bias=b1_sb[:, t : t + 1]
+                    )
+            nc.vector.tensor_copy(
+                h_bf[half][:].rearrange("p (c i t) -> p c t i", i=4, t=4),
+                h_rows[half][:].rearrange("p t (c i) -> p c t i", i=4),
+            )
+            nc.vector.quantize_mx(h_w[half][:].bitcast(FP8X4), h_s[half][:], h_bf[half][:])
+
+        wb_w = [
+            [held([P, BANK], U32, f"wb_w{a}0", f"w1_w{a}"), held([P, BANK], U32, f"wb_w{a}1", f"h_rows{a}")]
+            for a in range(2)
+        ]
+        wa_w = [held([P, BANK], U16, "wa_w0", "w1_s1"), held([P, BANK], U16, "wa_w1", "h_bf1")]
+
+        def deal(g):
+            cols = slice(BANK * g, BANK * (g + 1))
+            for a in range(2):
+                nc.scalar.copy(
+                    wb_w[a][g][:].rearrange("p (t c i) -> p c t i", t=4, i=4),
+                    wb_raw[a][:, cols].rearrange("p (c i t) -> p c t i", t=4, i=4),
+                )
+            nc.scalar.copy(
+                wa_w[g][:].rearrange("p (t c i) -> p c t i", t=4, i=8),
+                wa_raw[:, cols].rearrange("p (c i t) -> p c t i", t=4, i=8),
+            )
+
+        tops = held([P, 2 * TILES], F32, "tops")
+        shift = held([P, TILES], F32, "shift")
+        y = [held([P, 4, M], F32, f"y{g}") for g in range(2)]
+        y_bf = [held([P, 4 * M], BF16, f"y_bf{g}") for g in range(2)]
+        y_w = [held([P, M], U32, f"y_w{g}") for g in range(2)]
+        y_s = [held([P, M], U8, f"y_s{g}") for g in range(2)]
+        out_rows = out_0.rearrange("(g p t) m -> g p t m", p=P, t=4)
+        scores, gains = {}, {}
+
+        def score(r):
+            g, t = divmod(r, 4)
+            cols = slice(P * t, P * (t + 1))
+            s_cols = slice(P * r, P * (r + 1))
+            e = ring.tile([P, S], F32, name="e", align_bytes=64)
+            for half in range(2):
+                acc = psum.tile([P, BANK], F32, name="acc")
+                for a in range(2):
+                    nc.tensor.matmul_mx(
+                        out=acc[:],
+                        lhsT=wb_w[a][g][:, cols].bitcast(FP8X4),
+                        lhsT_scale=w_s[4 * (a + 1) : P, s_cols],
+                        start=(a == 0),
+                        stop=False,
+                        **v_operand(a, half),
+                    )
+                nc.tensor.matmul_mx(
+                    out=acc[:],
+                    lhsT=wa_w[g][:, cols].bitcast(FP4X4),
+                    lhsT_scale=w_s[:, s_cols],
+                    rhs=h_w[half][:].bitcast(FP8X4),
+                    rhs_scale=h_s[half][:],
+                    start=False,
+                    stop=True,
+                )
+                nc.vector.tensor_scalar(
+                    e[:, BANK * half : BANK * (half + 1)], acc[:], 1.0, None, ALU.mult, ALU.max,
+                    accum_out=tops[:, 2 * r + half : 2 * r + half + 1],
+                )
+            scores[r] = e
+
+        def look(r):
+            col = slice(r, r + 1)
+            nc.vector.tensor_scalar(
+                shift[:, col], tops[:, 2 * r : 2 * r + 1], tops[:, 2 * r + 1 : 2 * r + 2],
+                neg_temp[:, col], ALU.max, ALU.mult,
+            )
+            rival = ring.tile([P, M], F32, name="rival", align_bytes=64)
+            nc.scalar.activation(
+                rival[:], scores[r][:].indirect(p1[:]), ACT.Exp, bias=shift[:, col], scale=temp_sb[:, col]
+            )
+            gain = ring.tile([P, M], F32, name="gain", align_bytes=64)
+            if r < TILES - LAG:
+                nc.gpsimd.tensor_scalar(gain[:], rival[:], ga_sb[:, col], gc_sb[:, col], ALU.mult, ALU.add)
+            else:
+                nc.scalar.activation(gain[:], rival[:], ACT.Identity, bias=gc_sb[:, col], scale=ga_sb[:, col])
+            gains[r] = gain
+
+        def planes(g):
+            nc.vector.quantize_mx(y_w[g][:].bitcast(FP8X4), y_s[g][:], y_bf[g][:])
+            nc.sync.dma_start(
+                out_1[g].rearrange("p m t -> p (m t)").bitcast(I32), y_w[g][:].bitcast(I32)
+            )
+            for q in range(4):
+                eng = nc.sync if q % 2 == 0 else nc.scalar
+                eng.dma_start(
+                    out_2[g, 4 * q : 4 * q + 4, :].bitcast(I32),
+                    y_s[g][32 * q : 32 * q + 4, :].bitcast(I32),
+                )
+
+        def finish(r):
+            g, t = divmod(r, 4)
+            nc.vector.tensor_tensor(y[g][:, t, :], scores[r][:].indirect(p2[:]), gains[r][:], ALU.mult)
+            nc.sync.dma_start(out_rows[g, :, t, :], y[g][:, t, :])
+            dst = y_bf[g][:].rearrange("p (c i t) -> p c t i", i=4, t=4)
+            src = y[g][:].rearrange("p t (c i) -> p c t i", i=4)
+            if r == 3:
+                for c in range(2):
+                    nc.scalar.copy(dst[:, 64 * c : 64 * (c + 1)], src[:, 64 * c : 64 * (c + 1)])
+            if r == 5:
+                nc.scalar.copy(dst[:, :, 0:2], src[:, :, 0:2])
+            if r == 7:
+                nc.vector.tensor_copy(dst[:, :, 2:4], src[:, :, 2:4])
+
+        deal(0)
+        for step in range(TILES + LAG):
+            if step < TILES:
+                score(step)
+            if step == TILES - 1:
+                look(step)
+            if step >= LAG:
+                finish(step - LAG)
+            if step < TILES - 1:
+                look(step)
+            if step == 0:
+                deal(1)
+            if step == 4 + LAG:
+                planes(0)
+        planes(1)

@@ -49,10 +49,7 @@ def tile_list_page_flush_adviser_kernel(
         wb_raw = [held([P, N], U32, f"wb_raw{a}") for a in range(2)]
         wa_raw = held([P, N], U16, "wa_raw")
 
-        nc.vector.memset(tab_s[:].bitcast(I32), 0)
-        nc.gpsimd.memset(w_s_raw[:].bitcast(I32), 0)
-
-        nc.sync.dma_start(idx[:], offs)
+        nc.gpsimd.memset(tab_s[:].bitcast(I32), 0)
 
         def load_rows(dst, src):
             nc.sync.dma_start(
@@ -60,19 +57,13 @@ def tile_list_page_flush_adviser_kernel(
                 src.rearrange("(g p t) -> p g t", p=P, t=4),
             )
 
-        load_rows(temp_sb, temp)
-        load_rows(b1_sb, b1)
-        nc.sync.dma_start(p1[:], pos1)
-
         def load_words(dst, src):
             nc.sync.dma_start(dst[:].bitcast(I32), src.rearrange("p c i -> p (c i)").bitcast(I32))
 
         load_words(tab_w[0], tab_words[0])
-        for q in range(4):
-            nc.sync.dma_start(
-                tab_s[32 * q : 32 * q + 8, :].bitcast(I32),
-                tab_scales[:, 4 * q : 4 * q + 4, :].bitcast(I32),
-            )
+        nc.sync.dma_start(idx[:], offs)
+        load_rows(temp_sb, temp)
+        load_rows(b1_sb, b1)
         nc.sync.dma_start(w1_raw0[:], w1[0:512, :].rearrange("(p j) c -> p j c", j=4))
         load_words(tab_w[1], tab_words[1])
 
@@ -87,9 +78,16 @@ def tile_list_page_flush_adviser_kernel(
         for a in range(2):
             load_words(wb_raw[a], wb_words[a])
         nc.sync.dma_start(wa_raw[:].bitcast(I32), wa_words[0].bitcast(I32))
+        nc.sync.dma_start(p1[:], pos1)
         nc.sync.dma_start(p2[:], pos2)
         load_rows(ga_sb, ga)
         load_rows(gc_sb, gc)
+        for q in range(4):
+            nc.gpsimd.dma_start(
+                tab_s[32 * q : 32 * q + 8, :].bitcast(I32),
+                tab_scales[:, 4 * q : 4 * q + 4, :].bitcast(I32),
+            )
+        nc.gpsimd.memset(w_s_raw[:].bitcast(I32), 0)
         for q in range(4):
             nc.gpsimd.dma_start(
                 w_s_raw[32 * q : 32 * q + 4, :].bitcast(I32),
@@ -108,7 +106,7 @@ def tile_list_page_flush_adviser_kernel(
         nc.vector.tensor_copy(v_w[0][:], tab_w[0][:].indirect(idx[:]))
         nc.vector.tensor_copy(v_s[:], tab_s[:].indirect(idx[:]))
 
-        w1_w = [held([P, H], U32, f"w1_w{a}") for a in range(2)]
+        w1_w = [held([P, H], U32, "w1_w0", "tab_s"), held([P, H], U32, "w1_w1")]
         w1_s = [held([P, H], U8, f"w1_s{a}") for a in range(2)]
 
         def w1_views(bf, raw):
@@ -177,7 +175,7 @@ def tile_list_page_flush_adviser_kernel(
             nc.vector.quantize_mx(h_w[half][:].bitcast(FP8X4), h_s[half][:], h_bf[half][:])
 
         wb_w = [
-            [held([P, BANK], U32, f"wb_w{a}0", f"w1_w{a}"), held([P, BANK], U32, f"wb_w{a}1", f"h_rows{a}")]
+            [held([P, BANK], U32, f"wb_w{a}0", ("tab_s", "w1_w1")[a]), held([P, BANK], U32, f"wb_w{a}1", f"h_rows{a}")]
             for a in range(2)
         ]
         wa_w = [held([P, BANK], U16, "wa_w0", "w1_s1"), held([P, BANK], U16, "wa_w1", "h_bf1")]
@@ -201,7 +199,7 @@ def tile_list_page_flush_adviser_kernel(
         y_w = [held([P, M], U32, f"y_w{g}") for g in range(2)]
         y_s = [held([P, M], U8, f"y_s{g}") for g in range(2)]
         out_rows = out_0.rearrange("(g p t) m -> g p t m", p=P, t=4)
-        scores, gains = {}, {}
+        scores, rivals, gains = {}, {}, {}
 
         def score(r):
             g, t = divmod(r, 4)
@@ -244,11 +242,15 @@ def tile_list_page_flush_adviser_kernel(
             nc.scalar.activation(
                 rival[:], scores[r][:].indirect(p1[:]), ACT.Exp, bias=shift[:, col], scale=temp_sb[:, col]
             )
+            rivals[r] = rival
+
+        def weigh(r):
+            col = slice(r, r + 1)
             gain = ring.tile([P, M], F32, name="gain", align_bytes=64)
-            if r < TILES - LAG:
-                nc.gpsimd.tensor_scalar(gain[:], rival[:], ga_sb[:, col], gc_sb[:, col], ALU.mult, ALU.add)
+            if r == TILES - 1:
+                nc.vector.tensor_scalar(gain[:], rivals[r][:], ga_sb[:, col], gc_sb[:, col], ALU.mult, ALU.add)
             else:
-                nc.scalar.activation(gain[:], rival[:], ACT.Identity, bias=gc_sb[:, col], scale=ga_sb[:, col])
+                nc.scalar.activation(gain[:], rivals[r][:], ACT.Identity, bias=gc_sb[:, col], scale=ga_sb[:, col])
             gains[r] = gain
 
         def planes(g):
@@ -267,28 +269,28 @@ def tile_list_page_flush_adviser_kernel(
             g, t = divmod(r, 4)
             nc.vector.tensor_tensor(y[g][:, t, :], scores[r][:].indirect(p2[:]), gains[r][:], ALU.mult)
             nc.sync.dma_start(out_rows[g, :, t, :], y[g][:, t, :])
-            dst = y_bf[g][:].rearrange("p (c i t) -> p c t i", i=4, t=4)
-            src = y[g][:].rearrange("p t (c i) -> p c t i", i=4)
-            if r == 3:
-                for c in range(2):
-                    nc.scalar.copy(dst[:, 64 * c : 64 * (c + 1)], src[:, 64 * c : 64 * (c + 1)])
-            if r == 5:
-                nc.scalar.copy(dst[:, :, 0:2], src[:, :, 0:2])
-            if r == 7:
-                nc.vector.tensor_copy(dst[:, :, 2:4], src[:, :, 2:4])
+            if t % 2 == 1:
+                dst = y_bf[g][:].rearrange("p (m t) -> p m t", t=4)[:, :, t - 1 : t + 1]
+                src = y[g][:, t - 1 : t + 1, :].rearrange("p t m -> p m t")
+                if r == TILES - 1:
+                    nc.vector.tensor_copy(dst, src)
+                else:
+                    for c in range(2):
+                        nc.scalar.copy(dst[:, 256 * c : 256 * (c + 1)], src[:, 256 * c : 256 * (c + 1)])
 
         deal(0)
-        for step in range(TILES + LAG):
-            if step < TILES:
-                score(step)
-            if step == TILES - 1:
-                look(step)
+        deal(1)
+        for step in range(TILES - 1):
+            score(step)
             if step >= LAG:
                 finish(step - LAG)
-            if step < TILES - 1:
-                look(step)
-            if step == 0:
-                deal(1)
-            if step == 4 + LAG:
-                planes(0)
+            look(step)
+            weigh(step)
+        score(7)
+        look(7)
+        finish(5)
+        finish(6)
+        weigh(7)
+        planes(0)
+        finish(7)
         planes(1)

@@ -49,7 +49,8 @@ def tile_list_page_flush_adviser_kernel(
         wb_raw = [held([P, N], U32, f"wb_raw{a}") for a in range(2)]
         wa_raw = held([P, N], U16, "wa_raw")
 
-        nc.gpsimd.memset(tab_s[:].bitcast(I32), 0)
+        nc.gpsimd.memset(w_s_raw[:].bitcast(I32), 0)
+        nc.vector.memset(tab_s[:].bitcast(I32), 0)
 
         def load_rows(dst, src):
             nc.sync.dma_start(
@@ -60,9 +61,8 @@ def tile_list_page_flush_adviser_kernel(
         def load_words(dst, src):
             nc.sync.dma_start(dst[:].bitcast(I32), src.rearrange("p c i -> p (c i)").bitcast(I32))
 
-        load_words(tab_w[0], tab_words[0])
         nc.sync.dma_start(idx[:], offs)
-        load_rows(temp_sb, temp)
+        load_words(tab_w[0], tab_words[0])
         load_rows(b1_sb, b1)
         nc.sync.dma_start(w1_raw0[:], w1[0:512, :].rearrange("(p j) c -> p j c", j=4))
         load_words(tab_w[1], tab_words[1])
@@ -75,9 +75,15 @@ def tile_list_page_flush_adviser_kernel(
             return raw
 
         w1_raw1 = [load_w1_half(0), load_w1_half(1)]
+        for q in range(4):
+            nc.sync.dma_start(
+                w_s_raw[32 * q : 32 * q + 4, :].bitcast(I32),
+                wa_scales[0, 4 * q : 4 * q + 4, :].bitcast(I32),
+            )
         for a in range(2):
             load_words(wb_raw[a], wb_words[a])
         nc.sync.dma_start(wa_raw[:].bitcast(I32), wa_words[0].bitcast(I32))
+        load_rows(temp_sb, temp)
         nc.sync.dma_start(p1[:], pos1)
         nc.sync.dma_start(p2[:], pos2)
         load_rows(ga_sb, ga)
@@ -87,19 +93,11 @@ def tile_list_page_flush_adviser_kernel(
                 tab_s[32 * q : 32 * q + 8, :].bitcast(I32),
                 tab_scales[:, 4 * q : 4 * q + 4, :].bitcast(I32),
             )
-        nc.gpsimd.memset(w_s_raw[:].bitcast(I32), 0)
         for q in range(4):
-            nc.gpsimd.dma_start(
-                w_s_raw[32 * q : 32 * q + 4, :].bitcast(I32),
-                wa_scales[0, 4 * q : 4 * q + 4, :].bitcast(I32),
-            )
             nc.gpsimd.dma_start(
                 w_s_raw[32 * q + 4 : 32 * q + 12, :].bitcast(I32),
                 wb_scales[:, 4 * q : 4 * q + 4, :].bitcast(I32),
             )
-
-        neg_temp = held([P, TILES], F32, "neg_temp")
-        nc.vector.tensor_scalar(neg_temp[:], temp_sb[:], -1.0, None, ALU.mult)
 
         v_w = [held([P, S], U32, "v_w0")]
         v_s = held([P, S], U8, "v_s")
@@ -174,6 +172,9 @@ def tile_list_page_flush_adviser_kernel(
             )
             nc.vector.quantize_mx(h_w[half][:].bitcast(FP8X4), h_s[half][:], h_bf[half][:])
 
+        neg_temp = held([P, TILES], F32, "neg_temp", "h_bf0")
+        nc.vector.tensor_scalar(neg_temp[:], temp_sb[:], -1.0, None, ALU.mult)
+
         wb_w = [
             [held([P, BANK], U32, f"wb_w{a}0", ("tab_s", "w1_w1")[a]), held([P, BANK], U32, f"wb_w{a}1", f"h_rows{a}")]
             for a in range(2)
@@ -197,7 +198,7 @@ def tile_list_page_flush_adviser_kernel(
         y = [held([P, 4, M], F32, f"y{g}") for g in range(2)]
         y_bf = [held([P, 4 * M], BF16, f"y_bf{g}") for g in range(2)]
         y_w = [held([P, M], U32, f"y_w{g}") for g in range(2)]
-        y_s = [held([P, M], U8, f"y_s{g}") for g in range(2)]
+        y_s = held([P, M], U8, "y_s")
         out_rows = out_0.rearrange("(g p t) m -> g p t m", p=P, t=4)
         scores, rivals, gains = {}, {}, {}
 
@@ -205,7 +206,7 @@ def tile_list_page_flush_adviser_kernel(
             g, t = divmod(r, 4)
             cols = slice(P * t, P * (t + 1))
             s_cols = slice(P * r, P * (r + 1))
-            e = ring.tile([P, S], F32, name="e", align_bytes=64)
+            e = ring.tile([P, S], F32, name="e", bufs=4, align_bytes=64)
             for half in range(2):
                 acc = psum.tile([P, BANK], F32, name="acc")
                 for a in range(2):
@@ -253,30 +254,34 @@ def tile_list_page_flush_adviser_kernel(
                 nc.scalar.activation(gain[:], rivals[r][:], ACT.Identity, bias=gc_sb[:, col], scale=ga_sb[:, col])
             gains[r] = gain
 
-        def planes(g):
-            nc.vector.quantize_mx(y_w[g][:].bitcast(FP8X4), y_s[g][:], y_bf[g][:])
+        def planes(g, cols):
+            wide = slice(4 * cols.start, 4 * cols.stop)
+            nc.vector.quantize_mx(y_w[g][:, cols].bitcast(FP8X4), y_s[4 * g : P, cols], y_bf[g][:, wide])
             nc.sync.dma_start(
-                out_1[g].rearrange("p m t -> p (m t)").bitcast(I32), y_w[g][:].bitcast(I32)
+                out_1[g, :, cols, :].rearrange("p m t -> p (m t)").bitcast(I32), y_w[g][:, cols].bitcast(I32)
             )
-            for q in range(4):
-                eng = nc.sync if q % 2 == 0 else nc.scalar
-                eng.dma_start(
-                    out_2[g, 4 * q : 4 * q + 4, :].bitcast(I32),
-                    y_s[g][32 * q : 32 * q + 4, :].bitcast(I32),
-                )
+
+        def pick(r, cols):
+            g, t = divmod(r, 4)
+            entries = p2[:, cols.start // 16 : cols.stop // 16]
+            nc.vector.tensor_tensor(y[g][:, t, cols], scores[r][:].indirect(entries), gains[r][:, cols], ALU.mult)
+            nc.sync.dma_start(out_rows[g, :, t, cols], y[g][:, t, cols])
+
+        def pair_views(r, cols):
+            g, t = divmod(r, 4)
+            return (
+                y_bf[g][:].rearrange("p (m t) -> p m t", t=4)[:, cols, t - 1 : t + 1],
+                y[g][:, t - 1 : t + 1, cols].rearrange("p t m -> p m t"),
+            )
+
+        whole = slice(0, M)
+        halves = (slice(0, M // 2), slice(M // 2, M))
 
         def finish(r):
-            g, t = divmod(r, 4)
-            nc.vector.tensor_tensor(y[g][:, t, :], scores[r][:].indirect(p2[:]), gains[r][:], ALU.mult)
-            nc.sync.dma_start(out_rows[g, :, t, :], y[g][:, t, :])
-            if t % 2 == 1:
-                dst = y_bf[g][:].rearrange("p (m t) -> p m t", t=4)[:, :, t - 1 : t + 1]
-                src = y[g][:, t - 1 : t + 1, :].rearrange("p t m -> p m t")
-                if r == TILES - 1:
-                    nc.vector.tensor_copy(dst, src)
-                else:
-                    for c in range(2):
-                        nc.scalar.copy(dst[:, 256 * c : 256 * (c + 1)], src[:, 256 * c : 256 * (c + 1)])
+            pick(r, whole)
+            if r % 2 == 1:
+                for cols in halves:
+                    nc.scalar.copy(*pair_views(r, cols))
 
         deal(0)
         deal(1)
@@ -291,6 +296,14 @@ def tile_list_page_flush_adviser_kernel(
         finish(5)
         finish(6)
         weigh(7)
-        planes(0)
-        finish(7)
-        planes(1)
+        planes(0, whole)
+        for cols in halves:
+            pick(7, cols)
+        for cols in halves:
+            nc.vector.tensor_copy(*pair_views(7, cols))
+        for cols in halves:
+            planes(1, cols)
+        for q in range(4):
+            (nc.sync, nc.scalar)[q % 2].dma_start(
+                out_2[:, 4 * q : 4 * q + 4, :].bitcast(I32), y_s[32 * q : 32 * q + 8, :].bitcast(I32)
+            )

@@ -63,8 +63,14 @@ def tile_list_page_flush_adviser_kernel(
 
         nc.sync.dma_start(idx[:], offs)
         load_words(tab_w[0], tab_words[0])
-        load_rows(b1_sb, b1)
         nc.sync.dma_start(w1_raw0[:], w1[0:512, :].rearrange("(p j) c -> p j c", j=4))
+        load_rows(b1_sb, b1)
+        load_rows(temp_sb, temp)
+        for q in range(4):
+            nc.sync.dma_start(
+                tab_s[32 * q : 32 * q + 8, :].bitcast(I32),
+                tab_scales[:, 4 * q : 4 * q + 4, :].bitcast(I32),
+            )
         load_words(tab_w[1], tab_words[1])
 
         def load_w1_half(c):
@@ -75,29 +81,25 @@ def tile_list_page_flush_adviser_kernel(
             return raw
 
         w1_raw1 = [load_w1_half(0), load_w1_half(1)]
-        for q in range(4):
-            nc.sync.dma_start(
-                w_s_raw[32 * q : 32 * q + 4, :].bitcast(I32),
-                wa_scales[0, 4 * q : 4 * q + 4, :].bitcast(I32),
-            )
         for a in range(2):
             load_words(wb_raw[a], wb_words[a])
         nc.sync.dma_start(wa_raw[:].bitcast(I32), wa_words[0].bitcast(I32))
-        load_rows(temp_sb, temp)
         nc.sync.dma_start(p1[:], pos1)
         nc.sync.dma_start(p2[:], pos2)
         load_rows(ga_sb, ga)
         load_rows(gc_sb, gc)
         for q in range(4):
             nc.gpsimd.dma_start(
-                tab_s[32 * q : 32 * q + 8, :].bitcast(I32),
-                tab_scales[:, 4 * q : 4 * q + 4, :].bitcast(I32),
+                w_s_raw[32 * q : 32 * q + 4, :].bitcast(I32),
+                wa_scales[0, 4 * q : 4 * q + 4, :].bitcast(I32),
             )
-        for q in range(4):
             nc.gpsimd.dma_start(
                 w_s_raw[32 * q + 4 : 32 * q + 12, :].bitcast(I32),
                 wb_scales[:, 4 * q : 4 * q + 4, :].bitcast(I32),
             )
+
+        neg_temp = held([P, TILES], F32, "neg_temp")
+        nc.vector.tensor_scalar(neg_temp[:], temp_sb[:], -1.0, None, ALU.mult)
 
         v_w = [held([P, S], U32, "v_w0")]
         v_s = held([P, S], U8, "v_s")
@@ -128,12 +130,6 @@ def tile_list_page_flush_adviser_kernel(
                 nc.vector.quantize_mx(
                     w1_w[1][:, cols].bitcast(FP8X4), w1_s[1][:, cols], w1_bf1[c][:, 256 * t : 256 * (t + 1)]
                 )
-
-        w_s = held([P, N], U8, "w_s", "tab_w1")
-        nc.vector.tensor_copy(
-            w_s[:].rearrange("p (g t c i) -> p g c t i", g=2, t=4, i=16),
-            w_s_raw[:].rearrange("p (g c i t) -> p g c t i", g=2, t=4, i=16),
-        )
 
         def v_operand(a, half):
             cols = slice(BANK * half, BANK * (half + 1))
@@ -170,13 +166,16 @@ def tile_list_page_flush_adviser_kernel(
                 h_bf[half][:].rearrange("p (c i t) -> p c t i", i=4, t=4),
                 h_rows[half][:].rearrange("p t (c i) -> p c t i", i=4),
             )
+            if half == 0:
+                w_s = held([P, N], U8, "w_s", "h_rows0")
+                nc.vector.tensor_copy(
+                    w_s[:].rearrange("p (g t c i) -> p g c t i", g=2, t=4, i=16),
+                    w_s_raw[:].rearrange("p (g c i t) -> p g c t i", g=2, t=4, i=16),
+                )
             nc.vector.quantize_mx(h_w[half][:].bitcast(FP8X4), h_s[half][:], h_bf[half][:])
 
-        neg_temp = held([P, TILES], F32, "neg_temp", "h_bf0")
-        nc.vector.tensor_scalar(neg_temp[:], temp_sb[:], -1.0, None, ALU.mult)
-
         wb_w = [
-            [held([P, BANK], U32, f"wb_w{a}0", ("tab_s", "w1_w1")[a]), held([P, BANK], U32, f"wb_w{a}1", f"h_rows{a}")]
+            [held([P, BANK], U32, f"wb_w{a}0", ("tab_s", "w1_w1")[a]), held([P, BANK], U32, f"wb_w{a}1", ("h_bf0", "h_rows1")[a])]
             for a in range(2)
         ]
         wa_w = [held([P, BANK], U16, "wa_w0", "w1_s1"), held([P, BANK], U16, "wa_w1", "h_bf1")]
@@ -248,10 +247,7 @@ def tile_list_page_flush_adviser_kernel(
         def weigh(r):
             col = slice(r, r + 1)
             gain = ring.tile([P, M], F32, name="gain", align_bytes=64)
-            if r == TILES - 1:
-                nc.vector.tensor_scalar(gain[:], rivals[r][:], ga_sb[:, col], gc_sb[:, col], ALU.mult, ALU.add)
-            else:
-                nc.scalar.activation(gain[:], rivals[r][:], ACT.Identity, bias=gc_sb[:, col], scale=ga_sb[:, col])
+            nc.scalar.activation(gain[:], rivals[r][:], ACT.Identity, bias=gc_sb[:, col], scale=ga_sb[:, col])
             gains[r] = gain
 
         def planes(g, cols):
@@ -267,41 +263,36 @@ def tile_list_page_flush_adviser_kernel(
             nc.vector.tensor_tensor(y[g][:, t, cols], scores[r][:].indirect(entries), gains[r][:, cols], ALU.mult)
             nc.sync.dma_start(out_rows[g, :, t, cols], y[g][:, t, cols])
 
-        def pair_views(r, cols):
-            g, t = divmod(r, 4)
+        def round_views(g, cols):
             return (
-                y_bf[g][:].rearrange("p (m t) -> p m t", t=4)[:, cols, t - 1 : t + 1],
-                y[g][:, t - 1 : t + 1, cols].rearrange("p t m -> p m t"),
+                y_bf[g][:].rearrange("p (m t) -> p m t", t=4)[:, cols],
+                y[g][:, :, cols].rearrange("p t m -> p m t"),
             )
 
         whole = slice(0, M)
         halves = (slice(0, M // 2), slice(M // 2, M))
-
-        def finish(r):
-            pick(r, whole)
-            if r % 2 == 1:
-                for cols in halves:
-                    nc.scalar.copy(*pair_views(r, cols))
 
         deal(0)
         deal(1)
         for step in range(TILES - 1):
             score(step)
             if step >= LAG:
-                finish(step - LAG)
+                pick(step - LAG, whole)
             look(step)
             weigh(step)
         score(7)
         look(7)
-        finish(5)
-        finish(6)
         weigh(7)
+        for c in range(4):
+            nc.scalar.copy(*round_views(0, slice(P * c, P * (c + 1))))
+        pick(5, whole)
+        pick(6, whole)
         planes(0, whole)
         for cols in halves:
             pick(7, cols)
-        for cols in halves:
-            nc.vector.tensor_copy(*pair_views(7, cols))
-        for cols in halves:
+        nc.scalar.copy(*round_views(1, halves[0]))
+        nc.vector.tensor_copy(*round_views(1, halves[1]))
+        for cols in reversed(halves):
             planes(1, cols)
         for q in range(4):
             (nc.sync, nc.scalar)[q % 2].dma_start(

from contextlib import ExitStack

import concourse.mybir as mybir

K, T, S, H, N, M = 1024, 4096, 1024, 512, 1024, 512
FLOPS = 2 * (K * H * S + H * N * S + K * N * S)

F32 = mybir.dt.float32
BF16 = mybir.dt.bfloat16
I32 = mybir.dt.int32
U32 = mybir.dt.uint32
U16 = mybir.dt.uint16
U8 = mybir.dt.uint8
FP8X4 = mybir.dt.float8_e4m3fn_x4
FP4X4 = mybir.dt.float4_e2m1fn_x4
ALU = mybir.AluOpType
ACT = mybir.ActivationFunctionType

P = 128
BANK = 512
TILES = N // P
LAG = 2


def tile_list_page_flush_adviser_kernel(
    tc, tab_words, tab_scales, offs, pos1, pos2, w1, b1, wa_words, wa_scales,
    wb_words, wb_scales, temp, ga, gc, out_0, out_1, out_2,
):
    nc = tc.nc
    with ExitStack() as ctx:
        keep = ctx.enter_context(tc.tile_pool(name="keep", bufs=1))
        ring = ctx.enter_context(tc.tile_pool(name="ring", bufs=3))
        psum = ctx.enter_context(tc.psum_pool(name="psum", bufs=8))

        def held(shape, dtype, name, after=None):
            return keep.tile(shape, dtype, name=name, tag=after or name, align_bytes=64)

        idx = held([P, S // 16], U16, "idx")
        p1 = held([P, M // 16], U16, "p1")
        p2 = held([P, M // 16], U16, "p2")
        b1_sb = held([P, 4], F32, "b1_sb")
        temp_sb = held([P, TILES], F32, "temp_sb")
        ga_sb = held([P, TILES], F32, "ga_sb")
        gc_sb = held([P, TILES], F32, "gc_sb")
        tab_w = [held([P, T], U32, f"tab_w{a}") for a in range(2)]
        tab_s = held([P, T], U8, "tab_s")
        w_s_raw = held([P, N], U8, "w_s_raw")
        w1_raw0 = held([P, 4, H], F32, "w1_raw0")
        wb_raw = [held([P, N], U32, f"wb_raw{a}") for a in range(2)]
        wa_raw = held([P, N], U16, "wa_raw")

        nc.gpsimd.memset(w_s_raw[:].bitcast(I32), 0)
        nc.vector.memset(tab_s[:].bitcast(I32), 0)

        def load_rows(dst, src):
            nc.sync.dma_start(
                dst[:].rearrange("p (g t) -> p g t", t=4),
                src.rearrange("(g p t) -> p g t", p=P, t=4),
            )

        def load_words(dst, src):
            nc.sync.dma_start(dst[:].bitcast(I32), src.rearrange("p c i -> p (c i)").bitcast(I32))

        nc.sync.dma_start(idx[:], offs)
        load_words(tab_w[0], tab_words[0])
        nc.sync.dma_start(w1_raw0[:], w1[0:512, :].rearrange("(p j) c -> p j c", j=4))
        load_rows(b1_sb, b1)
        load_rows(temp_sb, temp)
        for q in range(4):
            nc.sync.dma_start(
                tab_s[32 * q : 32 * q + 8, :].bitcast(I32),
                tab_scales[:, 4 * q : 4 * q + 4, :].bitcast(I32),
            )
        load_words(tab_w[1], tab_words[1])

        def load_w1_half(c):
            raw = held([P, 4, H // 2], F32, f"w1_raw1{c}")
            nc.sync.dma_start(
                raw[:], w1[512:1024, 256 * c : 256 * (c + 1)].rearrange("(p j) c -> p j c", j=4)
            )
            return raw

        w1_raw1 = [load_w1_half(0), load_w1_half(1)]
        for a in range(2):
            load_words(wb_raw[a], wb_words[a])
        nc.sync.dma_start(wa_raw[:].bitcast(I32), wa_words[0].bitcast(I32))
        nc.sync.dma_start(p1[:], pos1)
        nc.sync.dma_start(p2[:], pos2)
        load_rows(ga_sb, ga)
        load_rows(gc_sb, gc)
        for q in range(4):
            nc.gpsimd.dma_start(
                w_s_raw[32 * q : 32 * q + 4, :].bitcast(I32),
                wa_scales[0, 4 * q : 4 * q + 4, :].bitcast(I32),
            )
            nc.gpsimd.dma_start(
                w_s_raw[32 * q + 4 : 32 * q + 12, :].bitcast(I32),
                wb_scales[:, 4 * q : 4 * q + 4, :].bitcast(I32),
            )

        neg_temp = held([P, TILES], F32, "neg_temp")
        nc.vector.tensor_scalar(neg_temp[:], temp_sb[:], -1.0, None, ALU.mult)

        v_w = [held([P, S], U32, "v_w0")]
        v_s = held([P, S], U8, "v_s")
        nc.vector.tensor_copy(v_w[0][:], tab_w[0][:].indirect(idx[:]))
        nc.vector.tensor_copy(v_s[:], tab_s[:].indirect(idx[:]))

        w1_w = [held([P, H], U32, "w1_w0", "tab_s"), held([P, H], U32, "w1_w1")]
        w1_s = [held([P, H], U8, f"w1_s{a}") for a in range(2)]

        def w1_views(bf, raw):
            return (
                bf[:].rearrange("p (t m j) -> p m t j", t=4, j=4),
                raw[:].rearrange("p j (m t) -> p m t j", t=4),
            )

        w1_bf0 = held([P, 4 * H], BF16, "w1_bf0")
        nc.scalar.copy(*w1_views(w1_bf0, w1_raw0))
        nc.vector.quantize_mx(w1_w[0][:].bitcast(FP8X4), w1_s[0][:], w1_bf0[:])

        v_w.append(held([P, S], U32, "v_w1", "w1_bf0"))
        nc.vector.tensor_copy(v_w[1][:], tab_w[1][:].indirect(idx[:]))
        w1_bf1 = [held([P, 2 * H], BF16, "w1_bf10"), held([P, 2 * H], BF16, "w1_bf11", "tab_w1")]
        nc.scalar.copy(*w1_views(w1_bf1[0], w1_raw1[0]))
        nc.vector.tensor_copy(*w1_views(w1_bf1[1], w1_raw1[1]))
        for c in range(2):
            for t in range(4):
                cols = slice(P * t + 64 * c, P * t + 64 * (c + 1))
                nc.vector.quantize_mx(
                    w1_w[1][:, cols].bitcast(FP8X4), w1_s[1][:, cols], w1_bf1[c][:, 256 * t : 256 * (t + 1)]
                )

        def v_operand(a, half):
            cols = slice(BANK * half, BANK * (half + 1))
            return dict(rhs=v_w[a][:, cols].bitcast(FP8X4), rhs_scale=v_s[4 * a : P, cols])

        h_acc = [[psum.tile([P, BANK], F32, name="acc") for t in range(4)] for half in range(2)]
        for a in range(2):
            for half in range(2):
                for t in range(4):
                    cols = slice(P * t, P * (t + 1))
                    nc.tensor.matmul_mx(
                        out=h_acc[half][t][:],
                        lhsT=w1_w[a][:, cols].bitcast(FP8X4),
                        lhsT_scale=w1_s[a][:, cols],
                        start=(a == 0),
                        stop=(a == 1),
                        **v_operand(a, half),
                    )
        h_w = [held([P, BANK], U32, f"h_w{half}") for half in range(2)]
        h_s = [held([P, BANK], U8, f"h_s{half}") for half in range(2)]
        h_rows = [held([P, 4, BANK], BF16, f"h_rows{half}") for half in range(2)]
        h_bf = [held([P, 4 * BANK], BF16, f"h_bf{half}") for half in range(2)]
        for half in range(2):
            for t in range(4):
                if half == 0 and t % 2 == 1:
                    nc.vector.tensor_scalar(
                        h_rows[half][:, t, :], h_acc[half][t][:], b1_sb[:, t : t + 1], 0.0, ALU.add, ALU.max
                    )
                else:
                    nc.scalar.activation(
                        h_rows[half][:, t, :], h_acc[half][t][:], ACT.Relu, bias=b1_sb[:, t : t + 1]
                    )
            nc.vector.tensor_copy(
                h_bf[half][:].rearrange("p (c i t) -> p c t i", i=4, t=4),
                h_rows[half][:].rearrange("p t (c i) -> p c t i", i=4),
            )
            if half == 0:
                w_s = held([P, N], U8, "w_s", "h_rows0")
                nc.vector.tensor_copy(
                    w_s[:].rearrange("p (g t c i) -> p g c t i", g=2, t=4, i=16),
                    w_s_raw[:].rearrange("p (g c i t) -> p g c t i", g=2, t=4, i=16),
                )
            nc.vector.quantize_mx(h_w[half][:].bitcast(FP8X4), h_s[half][:], h_bf[half][:])

        wb_w = [
            [held([P, BANK], U32, f"wb_w{a}0", ("tab_s", "w1_w1")[a]), held([P, BANK], U32, f"wb_w{a}1", ("h_bf0", "h_rows1")[a])]
            for a in range(2)
        ]
        wa_w = [held([P, BANK], U16, "wa_w0", "w1_s1"), held([P, BANK], U16, "wa_w1", "h_bf1")]

        def deal(g):
            cols = slice(BANK * g, BANK * (g + 1))
            for a in range(2):
                nc.scalar.copy(
                    wb_w[a][g][:].rearrange("p (t c i) -> p c t i", t=4, i=4),
                    wb_raw[a][:, cols].rearrange("p (c i t) -> p c t i", t=4, i=4),
                )
            nc.scalar.copy(
                wa_w[g][:].rearrange("p (t c i) -> p c t i", t=4, i=8),
                wa_raw[:, cols].rearrange("p (c i t) -> p c t i", t=4, i=8),
            )

        tops = held([P, 2 * TILES], F32, "tops")
        shift = held([P, TILES], F32, "shift")
        y = [held([P, 4, M], F32, f"y{g}") for g in range(2)]
        y_bf = [held([P, 4 * M], BF16, f"y_bf{g}") for g in range(2)]
        y_w = [held([P, M], U32, f"y_w{g}") for g in range(2)]
        y_s = held([P, M], U8, "y_s")
        out_rows = out_0.rearrange("(g p t) m -> g p t m", p=P, t=4)
        scores, rivals, gains = {}, {}, {}

        def score(r):
            g, t = divmod(r, 4)
            cols = slice(P * t, P * (t + 1))
            s_cols = slice(P * r, P * (r + 1))
            e = ring.tile([P, S], F32, name="e", bufs=4, align_bytes=64)
            for half in range(2):
                acc = psum.tile([P, BANK], F32, name="acc")
                for a in range(2):
                    nc.tensor.matmul_mx(
                        out=acc[:],
                        lhsT=wb_w[a][g][:, cols].bitcast(FP8X4),
                        lhsT_scale=w_s[4 * (a + 1) : P, s_cols],
                        start=(a == 0),
                        stop=False,
                        **v_operand(a, half),
                    )
                nc.tensor.matmul_mx(
                    out=acc[:],
                    lhsT=wa_w[g][:, cols].bitcast(FP4X4),
                    lhsT_scale=w_s[:, s_cols],
                    rhs=h_w[half][:].bitcast(FP8X4),
                    rhs_scale=h_s[half][:],
                    start=False,
                    stop=True,
                )
                nc.vector.tensor_scalar(
                    e[:, BANK * half : BANK * (half + 1)], acc[:], 1.0, None, ALU.mult, ALU.max,
                    accum_out=tops[:, 2 * r + half : 2 * r + half + 1],
                )
            scores[r] = e

        def look(r):
            col = slice(r, r + 1)
            nc.vector.tensor_scalar(
                shift[:, col], tops[:, 2 * r : 2 * r + 1], tops[:, 2 * r + 1 : 2 * r + 2],
                neg_temp[:, col], ALU.max, ALU.mult,
            )
            rival = ring.tile([P, M], F32, name="rival", align_bytes=64)
            nc.scalar.activation(
                rival[:], scores[r][:].indirect(p1[:]), ACT.Exp, bias=shift[:, col], scale=temp_sb[:, col]
            )
            rivals[r] = rival

        def weigh(r):
            col = slice(r, r + 1)
            gain = ring.tile([P, M], F32, name="gain", align_bytes=64)
            nc.scalar.activation(gain[:], rivals[r][:], ACT.Identity, bias=gc_sb[:, col], scale=ga_sb[:, col])
            gains[r] = gain

        def planes(g, cols):
            wide = slice(4 * cols.start, 4 * cols.stop)
            nc.vector.quantize_mx(y_w[g][:, cols].bitcast(FP8X4), y_s[4 * g : P, cols], y_bf[g][:, wide])
            nc.sync.dma_start(
                out_1[g, :, cols, :].rearrange("p m t -> p (m t)").bitcast(I32), y_w[g][:, cols].bitcast(I32)
            )

        def pick(r, cols):
            g, t = divmod(r, 4)
            entries = p2[:, cols.start // 16 : cols.stop // 16]
            nc.vector.tensor_tensor(y[g][:, t, cols], scores[r][:].indirect(entries), gains[r][:, cols], ALU.mult)
            nc.sync.dma_start(out_rows[g, :, t, cols], y[g][:, t, cols])

        def round_views(g, cols):
            return (
                y_bf[g][:].rearrange("p (m t) -> p m t", t=4)[:, cols],
                y[g][:, :, cols].rearrange("p t m -> p m t"),
            )

        whole = slice(0, M)
        halves = (slice(0, M // 2), slice(M // 2, M))

        deal(0)
        deal(1)
        for step in range(TILES - 1):
            score(step)
            if step >= LAG:
                pick(step - LAG, whole)
            look(step)
            weigh(step)
        score(7)
        look(7)
        weigh(7)
        for c in range(4):
            nc.scalar.copy(*round_views(0, slice(P * c, P * (c + 1))))
        pick(5, whole)
        pick(6, whole)
        planes(0, whole)
        for cols in halves:
            pick(7, cols)
        nc.scalar.copy(*round_views(1, halves[0]))
        nc.vector.tensor_copy(*round_views(1, halves[1]))
        for cols in reversed(halves):
            planes(1, cols)
        for q in range(4):
            (nc.sync, nc.scalar)[q % 2].dma_start(
                out_2[:, 4 * q : 4 * q + 4, :].bitcast(I32), y_s[32 * q : 32 * q + 8, :].bitcast(I32)
            )
